import numpy as np, ml_dtypes
CORES = [40,41,42,43,44,45,46,47]
N = 8
BF = ml_dtypes.bfloat16
def gentries(a):
    return np.ascontiguousarray(a.reshape(8, 16, -1).transpose(0, 2, 1)).reshape(8, -1)
def gtable(e):
    e = np.asarray(e); return np.ascontiguousarray(e.reshape(8, -1, 16).transpose(0, 2, 1)).reshape(128, -1).astype(np.int32)
V, T, J, CAP, RO, M, LN = 2048, 512, 2, 64, 2, 4, 3
E = N * CAP * J; A = V + RO * E; F = 2 * J + 2
def codes(rng, back):
    u = rng.random((N, 8, 16, T))
    c = np.where(u < 0.15, 0, np.where(u < 0.5, rng.integers(1, J + 1, u.shape), J + back))
    c[:, :, F:] = 0; c[:, :, F] = rng.integers(1, J + 1, (N, 8, T))
    return c
def parts(rng):
    x = rng.integers(0, 16, (N, 8, 16, V)); kd = np.where(rng.random((N, 8, 2, V)) < 0.25, A, rng.integers(0, V, (N, 8, 2, V)))
    wt = rng.integers(0, 256, (N, 8, 16)); wt[..., 0] |= 1
    th = rng.integers(40, 81, (N, 8))
    for q in range(N):
        o = rng.permutation(8); th[q, o[0]] = 42; th[q, o[1]] = 80
    rx = rng.integers(0, 16, (N, 8, 16, T)); nx = rng.integers(0, 16, (N, 8, 16, J, T)); tk = codes(rng, rng.integers(1, V + 1, (N, 8, 16, T)))
    return x, kd, wt, th, rx, nx, tk
def small(a, n):
    return np.ascontiguousarray(a.reshape(N, 128, n)).astype(np.float32).astype(BF)
def pack(x, kd, wt, th, rx, nx, tk):
    return {"x0": small(x, V), "k0": np.stack([gtable(a) for a in kd[:, :, 0]]), "k1": np.stack([gtable(a) for a in kd[:, :, 1]]),
            "wt": wt.reshape(N, 128, 1).astype(np.int32), "th": np.repeat(th, 16, axis=1).reshape(N, 128, 1).astype(np.int32),
            "rx": small(rx, T), "nx": small(nx, J * T), "tk": np.ascontiguousarray(tk.reshape(N, 128, T)).astype(np.int32)}
def setup_inputs(rng):
    return pack(*parts(rng))
def setup_inputs_alike(rng):
    x, kd, wt, th, rx, nx, tk = parts(rng); v = np.arange(V)
    wt[:, ::2] = 0; th[:, ::2] = 70; th[:, ::4] = 241; th[:, 5] = 241
    kd[:, 1] = v; kd[:, 2, 0] = 0; kd[:, 2, 1] = V - 1; kd[:, 3] = np.where(v < V - 1, v + 1, A)
    x[:, 5] = np.tile(x[:, 5, :, :4], (1, 1, V // 4))
    tk[:, 4, :F] = 0; tk[:, 5, :F] = 1; tk[:, 6, :F] = rng.choice(np.array([J + 1, J + V]), (N, F, T)); tk[:, 7, :F] = rng.integers(1, J + 1, (N, F, T))
    tk[:, 0, F] = 1; tk[:, 1, F] = J
    return pack(x, kd, wt, th, rx, nx, tk)
def setup_inputs_edge(rng):
    x, kd, wt, th, rx, nx, tk = parts(rng)
    rho = rng.integers(2, 6, (8, 16)); th = rng.integers(8, 21, (N, 8))
    rx = np.broadcast_to(rho[None, :, :, None], (N, 8, 16, T)).copy(); rx[:, :, 0] += (rng.random((N, 8, T)) < 0.7).astype(np.int64)
    want = th[:, :, None] - 1 + rng.choice(np.array([-1, 0, 0, 1]), (N, 8, E))
    e = np.argsort(rng.random((N, 8, E, 30)), axis=-1) < want[..., None]
    e = np.add.reduce(e.reshape(N, 8, E, 15, 2).astype(np.int64), axis=-1)
    y = np.broadcast_to(rho[None, :, None, :], (N, 8, E, 16)).copy(); y[..., 1:] += e * rng.choice(np.array([-1, 1]), e.shape)
    x[..., V - E:] = 2 * y.transpose(0, 1, 3, 2) + rng.integers(0, 2, (N, 8, 16, E)); kd[..., V - E:] = A
    nx = rho[None, :, :, None, None] + rng.integers(-1, 2, (N, 8, 16, J, T))
    far = [int(g) for g in rng.permutation(8)[:3]]
    for g in far: kd[:, g, :, V - E:] = np.arange(V - E, V)
    for i in (0, 1):
        g = far[i]; lv = rng.integers(10, 15, N)
        if i == 0: lv[:] = 14
        x[:, g, :, V - E:] = lv[:, None, None] + rng.integers(-1, 2, (N, 16, E)); rx[:, g] = rng.integers(0, 4, (N, 16, T))
        th[:, g] = 16 * lv - 24 + rng.choice(np.array([-5, -3, -1, 1, 3, 5]), N)
    g = far[2]; few = rng.random((N, 1, E)) < 0.5
    x[:, g, :, V - E:] = np.where(few & (rng.random((N, 16, E)) < 0.2), 14, 15); x[:, g, :, V - E] = 15; rx[:, g] = 0
    th[:, g] = np.where(rng.permutation(N) % 2 == 0, 241, 240)
    wt[:, far[0]] = rng.integers(240, 256, (N, 16)); wt[:, far[2]] = rng.integers(240, 256, (N, 16))
    return pack(x, kd, wt, th, rx, nx, tk)
def setup_inputs_quiet(rng):
    x, kd, wt, th, rx, nx, tk = parts(rng)
    q = rng.permutation(N); th[q[1]] = 241; th[:, rng.integers(0, 8)] = 0; th[q[0]] = 0
    return pack(x, kd, wt, th, rx, nx, tk)
def setup_inputs_room(rng):
    x, kd, wt, th, rx, nx, tk = parts(rng)
    wt[:] = 0; wt[..., 0] = 1; wt[..., 1] = 8; wt[..., 2] = 64
    rx[:, :, 3:] = 0; th[:] = 50; kd[..., V - E:] = A
    for q in range(N):
        for g in range(8):
            n = rng.choice(np.array([0, 1, CAP - 1, CAP, CAP + 1, 2 * CAP]), N)
            if q == 0: n[1] = (CAP, CAP + 1, 0, CAP - 1, 1, 2 * CAP, CAP, CAP + 1)[g]
            own = np.concatenate([np.repeat(np.arange(N), n), np.full(E - int(np.sum(n)), -1)])
            own = rng.permutation(own)
            y = rng.integers(0, 8, (16, E)); y[3:] = np.where(own >= 0, 0, rng.integers(4, 8, (13, E)))
            y[0] = np.where(own >= 0, own + N * rng.integers(0, 8 // N, E), y[0])
            x[q, g, :, V - E:] = 2 * y + rng.integers(0, 2, (16, E))
    return pack(x, kd, wt, th, rx, nx, tk)
def setup_inputs_spread(rng):
    x, kd, wt, th, rx, nx, tk = parts(rng)
    x = np.floor(np.exp2(4 * rng.random((N, 8, 1, V))) * rng.random(x.shape)).astype(np.int64)
    rx = np.floor(np.exp2(4 * rng.random((N, 8, 1, T))) * rng.random(rx.shape)).astype(np.int64)
    nx = np.floor(np.exp2(4 * rng.random((N, 8, 1, J, T))) * rng.random(nx.shape)).astype(np.int64)
    wt = np.floor(np.exp2(8 * rng.random(wt.shape)) * rng.random(wt.shape)).astype(np.int64); wt[..., 0] |= 1
    th = np.where(rng.random((N, 8)) < 0.25, rng.integers(0, 242, (N, 8)), rng.integers(20, 80, (N, 8)))
    kd = np.where(rng.random(kd.shape) < 0.2, A, np.floor(V * rng.random(kd.shape) ** 3).astype(np.int64))
    tk = codes(rng, 1 + np.floor(V * rng.random((N, 8, 16, T)) ** 3).astype(np.int64))
    return pack(x, kd, wt, th, rx, nx, tk)
def check_inputs(d):
    bad = []
    for k in ("x0", "rx", "nx"):
        a = d[k].astype(np.float32)
        if not np.all((a >= 0) & (a <= 15) & (a == np.floor(a))): bad.append("range of " + k)
    for k in ("k0", "k1"):
        a = d[k]
        if not np.all(((a >= 0) & (a < V)) | (a == A)): bad.append("range of " + k)
    if np.min(d["wt"]) < 0 or np.max(d["wt"]) > 255: bad.append("range of wt")
    if np.min(d["th"]) < 0 or np.max(d["th"]) > 241: bad.append("range of th")
    a = d["th"].reshape(-1, 8, 16)
    if not np.all(a == a[:, :, :1]): bad.append("th alike in a group")
    a = d["tk"].reshape(-1, 8, 16, T)
    if np.min(a[:, :, :F]) < 0 or np.max(a[:, :, :F]) > J + V: bad.append("kid codes of tk")
    if np.min(a[:, :, F]) < 1 or np.max(a[:, :, F]) > J: bad.append("feet of tk")
    if np.any(a[:, :, F + 1:] != 0): bad.append("unused rows of tk")
    return bad
def pick(a, ix):
    return np.take_along_axis(a, ix[:, None, :], 2)
def sweep(x, kd, S):
    a, b = kd[:, 0, :S], kd[:, 1, :S]
    m = np.maximum(pick(x, a), pick(x, b))
    for u in (a, b):
        for i in range(2):
            m = np.maximum(m, pick(x, pick(kd[:, i:i + 1], u)[:, 0]) - 2)
    x[:, :, :S] = (x[:, :, :S] + m) >> 1
def whole_of(a):
    return a.astype(np.float32).astype(np.int64)
def reference(x0, k0, k1, wt, th, rx, nx, tk):
    X = np.zeros((N, 8, 16, A + 1), np.int64); X[..., :V] = whole_of(x0).reshape(N, 8, 16, V)
    K = np.full((N, 8, 2, A + 1), A, np.int64)
    for q in range(N):
        K[q, :, 0, :V] = gentries(k0[q]); K[q, :, 1, :V] = gentries(k1[q])
    ws = wt.astype(np.int64).reshape(N, 8, 16, 1); lim = th.astype(np.int64).reshape(N, 8, 16)[:, :, :1]
    rt = whole_of(rx).reshape(N, 8, 16, T); nd = whole_of(nx).reshape(N, 8, 16, J, T); rec = tk.astype(np.int64).reshape(N, 8, 16, T)
    roots = np.ascontiguousarray(rt.transpose(1, 2, 3, 0)).reshape(8, 16, T * N)
    live = np.ones((N, 8, E), bool)
    for t in range(RO):
        S = V + E * t; fresh = np.zeros((N, 8, E), bool)
        for q in range(N):
            sweep(X[q], K[q], S)
            x = X[q][:, :, S - E:S].copy(); h = np.add.reduce(ws[q] * x, axis=1)
            took = np.full((8, E), -1, np.int64)
            for m in range(M):
                c = (h + 97 * m + 31 * t) & (T * N - 1)
                dist = np.add.reduce(np.abs(x - pick(roots, c)), axis=1)
                took = np.where((took < 0) & live[q] & (dist < lim[q]), c, took)
            for g in range(8):
                xg, kg = X[q, g], K[q, g]
                for o in range(N):
                    i = np.flatnonzero((took[g] >= 0) & ((took[g] & (N - 1)) == o))[:CAP]
                    if len(i) == 0: continue
                    s = took[g, i] >> LN; v = S - E + i; k = CAP * o + np.arange(len(i)); b = S + J * k
                    oldx = xg[:, v].copy(); oldk = kg[:, v].copy(); cd = rec[o, g][:, s]
                    back = v - (cd - J); back = np.where(back < 0, back + S, back)
                    new = np.where(cd == 0, A, np.where(cd <= J, b + cd - 1, back))
                    for j in range(1, J + 1):
                        foot = cd[F] == j
                        xg[:, b + j - 1] = np.where(foot, oldx, nd[o, g, :, j - 1][:, s])
                        kg[:, b + j - 1] = np.where(foot, oldk, new[2 * j:2 * j + 2])
                        fresh[q, g, J * k + j - 1] = True
                    kg[:, v] = new[0:2]
                    xg[:, v] = (oldx + rt[o, g][:, s]) >> 1
        live = fresh
    for q in range(N): sweep(X[q], K[q], A)
    return {"y": np.ascontiguousarray(X[..., :A]).reshape(N, 128, A).astype(np.float32).astype(BF)}

import numpy as np
from concourse.bass import DstId, RemoteDMATransfer
from concourse.mybir import AluOpType as OP, ActivationFunctionType as AF

N, V, E, A = 8, 2048, 1024, 4096
OFF = 208.0
MAGIC = 12582912.0
XN = 16 + 2 * A
RT = XN + E
LIFT = 64.0

B, F, I, U, H = "bfloat16", "float32", "int32", "uint16", "float16"
SB = {
    "X0": (2064, B), "M0": (2064, B), "X": (4112, B), "M": (4112, B), "Y": (4096, B),
    "GA": (4096, B), "C": (4096, B), "MP": (4096, B),
    "kin": (256, I), "KA0": (128, U), "KA1": (128, U), "K0": (256, U), "K1": (256, U), "Kh": (128, H), "Kf": (128, F),
    "NW": (RT + A, B), "TK": (5120, F), "RG": (1024, B), "tki": (512, I), "wti": (8, I), "thi": (8, I),
    "D": (4096, B), "AD": (4096, B), "G": (1024, F), "Q": (1024, F), "W0": (1536, F), "W1": (1536, F), "W16": (512, H),
    "EX": (1024, B), "XC": (1024, B),
    "ones": (512, B), "ident": (128, B), "halfI": (128, B), "halfJ": (128, B), "epsI": (128, B), "negI": (128, B),
    "thI": (128, B), "BO": (128, B), "BT": (128, B), "UT": (128, B), "UU": (128, B),
    "Z1": (144, B), "Zt": (16, B), "Zw": (144, B), "Zn": (144, B), "ZG": (144, F),
    "RS64": (256, B), "RS8": (512, B),
    "jlo": (512, B), "jhi": (1024, B), "cf": (256, B), "cb": (1024, B),
    "pi": (8, I), "col": (16, F), "jl": (64, F), "j16": (64, F), "dump": (64, F),
    "ci": (256, I), "cj": (256, I), "Lr": (256, U), "pidx": (320, F), "best": (320, F),
    "qi": (192, I), "bi": (64, I), "ow": (64, I), "li": (64, I), "II": (512, B), "IC": (512, B), "own": (512, F),
    "Lc": (64, U), "Ld": (64, U), "Lk": (64, U), "Lx": (64, U), "sm": (640, F), "live": (64, B),
    "V2": (256, F), "Bm": (256, F), "keep": (256, F), "s1": (256, F), "s2": (256, F), "s3": (256, F),
}
SCRATCH = {k: ("sbuf", [128, v[0]], v[1]) for k, v in SB.items()}
SCRATCH["ZZ"] = ("sbuf", [128, 16, 144], B)
SCRATCH["ZP"] = ("sbuf", [128, 7, 144], B)
for _b in range(8):
    SCRATCH["P%d" % _b] = ("psum", [128, 512], F)
SEMAPHORES = ["ev", "ea", "ep", "eg", "lxa", "lxb", "lk0", "lk1", "lr", "ln1", "ln2", "lt", "lw", "lh",
              "aR", "aT", "aN", "sR", "sT", "sN", "ys", "c0", "c1", "c2", "c3"]

PAR = {"cyc": 1.04, "gam": 1.56, "sig": 3.8, "pec": 0.52, "mm": 20.0, "latx": 120.0, "lats": 60.0,
       "fix": {"v": 60.0, "a": 75.0, "p": 40.0, "g": 150.0, "s": 60.0},
       "relu": (True, True), "ch": 512, "adist": (2, 2), "nch": 256, "hsplit": ((0, 64), (64, 256)),
       "yrelu": (384,), "iters": 30000, "temp": 300.0, "seed": 2}


def build(g, core, T, topo):
    rank = T.rank_of(core)
    ops = []
    v, a, pe = g.vector, g.scalar, g.tensor
    GAM, SIG = PAR["gam"], PAR["sig"]

    def add(eng, fn, rd, wr, cyc, sem=None, cnt=0, lat=0.0, ns=None):
        ops.append({"e": eng, "fn": fn, "r": rd, "w": wr, "sem": sem, "cnt": cnt, "lat": lat,
                    "d": ns if ns is not None else PAR["fix"][eng] + max(cyc, 64) * PAR["cyc"]})

    def S(name, lo=0, hi=None, step=1, part=None):
        if hi is None:
            hi = SCRATCH[name][1][-1]
        p = slice(None) if part is None else slice(part[0], part[1])
        return (T[name][p, lo:hi:step] if step != 1 else T[name][p, lo:hi], (name, lo, hi), len(range(lo, hi, step)),
                SCRATCH[name][2], SCRATCH[name][0])

    def S3(name, f, lo, hi):
        return (T[name][:, f, lo:hi], (name, 0, 1), hi - lo, SCRATCH[name][2], "sbuf")

    def narrow(*xs):
        return all(x[3] in (B, H, U) for x in xs)

    def sc(x):
        return x[0] if isinstance(x, tuple) else x

    def regs(*xs):
        return [x[1] for x in xs if isinstance(x, tuple)]

    def ts(out, x, s1, o1, s2=None, o2=None):
        def fn():
            if o2 is None:
                return v.tensor_scalar(out[0], x[0], sc(s1), None, o1)
            return v.tensor_scalar(out[0], x[0], sc(s1), sc(s2), o1, o2)
        add("v", fn, regs(x, s1, s2), [out[1]], x[2] * (0.5 if narrow(out, x) else 1))

    def cp(out, x):
        add("v", lambda: v.tensor_copy(out[0], x[0]), [x[1]], [out[1]], x[2] * (0.5 if narrow(out, x) else 1))

    def tt(out, x, y, o):
        add("v", lambda: v.tensor_tensor(out[0], x[0], y[0], o), [x[1], y[1]], [out[1]],
            x[2] * (2 if x[4] == "sbuf" and y[4] == "sbuf" else 1))

    def ms(out, c):
        add("v", lambda: v.memset(out[0], c), [], [out[1]], out[2] * (0.5 if narrow(out) else 1))

    def scan(out, d0, d1, o0, o1):
        add("v", lambda: v.tensor_tensor_scan(out[0], d0[0], d1[0], 0.0, o0, o1), [d0[1], d1[1]], [out[1]],
            out[2] * (0.5 if narrow(out, d0, d1) else 1))

    def gtt(out, win, off, y, o):
        add("v", lambda: v.tensor_tensor(out[0], win[0].indirect(off[0]), y[0], o), [win[1], off[1], y[1]], [out[1]],
            out[2] * GAM)

    def act(out, x, f, bias=0.0, scale=1.0, off=None):
        def fn():
            src = x[0] if off is None else x[0].indirect(off[0])
            if f == AF.Copy:
                return a.activation(out[0], src, f)
            return a.activation(out[0], src, f, bias=sc(bias), scale=sc(scale))
        add("a", fn, regs(x, off, bias, scale), [out[1]], out[2] * (1 if off is None else GAM))

    def aff(out, x, mul, plus):
        act(out, x, AF.Identity, bias=plus, scale=mul)

    def mm(items, start=True, stop=True):
        def fn():
            last = None
            for n, it in enumerate(items):
                last = pe.matmul(it[0][0], it[1][0], it[2][0], start and n == 0, stop and n == len(items) - 1)
            return last
        cost = sum(PAR["mm"] + max(64, it[2][2]) * (4 if it[2][3] == F else 1) * PAR["pec"] for it in items)
        rd = []
        for it in items:
            rd += [it[1][1], it[2][1]]
        add("p", fn, sorted(set(rd)), sorted(set(it[0][1] for it in items)), 0, ns=PAR["fix"]["p"] + cost)

    def iota(out, pat, base, cm, n=None):
        def fn():
            if out[3] == I:
                return g.iota(out[0], pat, base, cm)
            return g.iota(out[0], pat, base, cm, allow_small_or_imprecise_dtypes=True)
        add("g", fn, [], [out[1]], 2 * (n or out[2]))

    def fill(out, c):
        iota(out, [[0, out[2]]], c, 0)

    def sel(out, x, pat, cmp, base, cm, n=None):
        add("g", lambda: g.affine_select(out[0], x[0], pat, cmp, 0.0, base, cm), [x[1]], [out[1]], 2 * (n or out[2]))

    def load(q, out, src, sem, lat, rd=()):
        eng = g.sync if q == "s" else a
        add(q, lambda: eng.dma_start(out[0], src), list(rd), [out[1], ("order" + q, 0, 1)], 0, sem=sem, cnt=16, lat=lat,
            ns=60.0)

    def whole(name):
        return (T[name][:], (name, 0, 1), 0, SCRATCH[name][2], "sbuf")

    def withdep(name):
        ops[-1]["r"] = ops[-1]["r"] + [(name, 0, 1)]

    def inorder(name):
        ops[-1]["w"] = ops[-1]["w"] + [(name, 0, 1)]

    o0 = 512 * rank
    load("s", S("kin", 0, 128), T.k0[:], "lk0", 2200)
    load("a", S("kin", 128, 256), T.k1[:], "lk1", 2200)
    load("s", S("X0", 0, 1024), T.x0[:, 0:1024], "lxa", 3000)
    load("a", S("X0", 1024, 2048), T.x0[:, 1024:2048], "lxb", 3000)
    load("s", S("NW", RT + o0, RT + o0 + 512), T.rx[:], "lr", 3400)
    load("s", S("tki"), T.tk[:], "lt", 4000)
    load("s", S("wti", 0, 1), T.wt[:], "lw", 4000)
    load("s", S("thi", 0, 1), T.th[:], "lh", 4000)
    load("s", S("NW", 16 + o0, 16 + o0 + 512), T.nx[:, 0:512], "ln1", 4500)
    load("s", S("NW", 16 + A + o0, 16 + A + o0 + 512), T.nx[:, 512:1024], "ln2", 4500)

    ones = S("ones")
    ms(ones, 1.0)
    ms(S("X0", 2048, 2064), 0.0)
    ms(S("M0", 2048, 2064), 0.0)
    row = (0, 1)
    iota(S("jlo", part=row), [[0, 2], [1, 256]], 0, 0)
    iota(S("jhi", 0, 512, part=row), [[256, 2], [0, 256]], 0, 0)
    iota(S("jhi", 512, 1024, part=row), [[256, 2], [0, 256]], 512, 0)
    sel(S("ident"), S("ones", 0, 128), [[-1, 128]], OP.is_equal, 0, 1)
    ident = S("ident")
    aff(S("halfI"), ident, 0.5, 0.0)
    aff(S("halfJ"), ident, 0.5 - 2.0 ** -9, 0.0)
    aff(S("epsI"), ident, 1.0 + 2.0 ** -7, 0.0)
    aff(S("negI"), ident, -1.0, 0.0)
    ms(S("cf", part=row), 0.0)
    ms(S("cf", 7, 128, 16, row), 1.0)
    ms(S("cf", 138, 256, 16, row), 1.0)
    L7, L10 = S("cf", 0, 128, part=row), S("cf", 128, 256, part=row)
    ms(S("cb", 0, 128, part=row), LIFT)
    ms(S("cb", 128, 256, part=row), 0.0)
    ms(S("cb", 8, 128, 16, row), 2048.0 + LIFT)
    ms(S("cb", 9, 128, 16, row), 2048.0 + LIFT)
    ms(S("cb", 138, 256, 16, row), float(o0))
    ms(S("cb", 256, 384, part=row), 2.0)
    ms(S("cb", 384, 512, part=row), MAGIC)
    ms(S("cb", 512, 640, part=row), -1.25)
    fill(S("cb", 768, 1024, part=row), 2048)
    L89, L10r, c2, cmag, c125 = [S("cb", 128 * n, 128 * n + 128, part=row) for n in range(5)]
    one1 = S("ones", 0, 128, part=row)

    def onerow(n):
        return S("ones", 0, n, part=row)

    ms(S("Z1"), 0.0)
    sel(S("Zt", 0, 8), S("ones", 0, 8), [[-16, 8]], OP.is_ge, 0, 1)
    sel(S("Z1", 15, 143, 16), S("Zt", 0, 8), [[16, 8]], OP.is_ge, 15, -1)
    cp(S("col", 0, 1), S("wti", 0, 1))
    ts(S("col", 1, 2), S("thi", 0, 1), 65536.0, OP.mult)
    aff(S("Zw"), S("Z1"), S("col", 0, 1), 0.0)
    aff(S("Zn"), S("Z1"), -65536.0, 0.0)
    aff(S("thI"), ident, S("col", 1, 2), 0.0)
    zz, zp = whole("ZZ"), whole("ZP")
    add("v", lambda: v.memset(T.ZZ[:], 0.0), [], [zz[1]], 1152)
    iota(zp, [[0, 1008]], 0, 0, n=1008)

    def sel3(z, f0, f1, c0, base):
        out = (T[z[1][0]][:, f0:f1, c0:c0 + 128:16], z[1])
        sel(out, S("ones", 0, 8 * (f1 - f0)), [[-1, f1 - f0], [-16, 8]], OP.is_equal, base, 1, n=8 * (f1 - f0))
    sel3(zz, 0, 16, 15, 0)
    aff(S("ZG"), S3("ZZ", 1, 0, 144), 4096.0, 0.0)
    tt(S("ZG"), S("ZG"), S3("ZZ", 0, 0, 144), OP.add)
    sel3(zp, 0, 5, 14, -6)
    sel3(zp, 0, 5, 15, -6)
    sel3(zp, 5, 7, 14, -2)
    sel3(zp, 5, 7, 15, -4)
    sel(S("BT"), S("ones", 0, 128), [[-16, 8], [0, 16]], OP.is_ge, 0, 1)
    sel(S("BO"), S("BT"), [[16, 8], [0, 16]], OP.is_ge, 15, -1)
    sel(S("UU"), S("BO"), [[-1, 128]], OP.is_gt, 0, 1)
    aff(S("BT"), ident, -2048.0, 0.0)
    tt(S("UT"), S("BT"), S("UU"), OP.subtract)
    fill(S("pidx", 0, 320, 5), 0)
    sel(S("RS64"), S("ones", 0, 256), [[0, 4], [1, 64]], OP.is_gt, 0, 0)
    sel(S("RS8"), ones, [[0, 64], [1, 8]], OP.is_gt, 0, 0)
    iota(S("pi", 0, 1), [[0, 1]], 0, 1)
    iota(S("j16"), [[16, 64]], 0, 0)
    ts(S("pi", 1, 2), S("pi", 0, 1), 15, OP.bitwise_and)
    ts(S("pi", 2, 3), S("pi", 0, 1), 1, OP.bitwise_and)
    cp(S("col", 2, 3), S("pi", 1, 2))
    cp(S("col", 3, 4), S("pi", 2, 3))
    aff(S("col", 4, 5), S("col", 3, 4), 1.0, 1.0)
    aff(S("col", 5, 6), S("col", 3, 4), float(A), 16.0)
    aff(S("col", 6, 7), S("col", 3, 4), -1.0, 0.0)
    jl = S("jl")
    aff(jl, S("j16"), 1.0, S("col", 2, 3))
    aff(S("dump"), jl, 1.0, 512.0)
    aff(S("j16"), jl, 1.0, S("col", 6, 7))
    fill(S("TK", 0, 1024), 0)
    fill(S("NW", 0, 16), 0)
    fill(S("W0", 0, 512), int(LIFT))
    fill(S("X", 3072, 4112), int(OFF))
    fill(S("M", 3072, 4112), int(OFF))
    fill(S("W1", 0, 512), int(LIFT))

    for b in range(2):
        ts(S("KA%d" % b), S("kin", 128 * b, 128 * b + 128), float(V), OP.min)
    for b in range(2):
        cp(S("K%d" % b, 0, 64), S("kin", 128 * b, 128 * b + 64))
        cp(S("Kf", 64 * b, 64 * b + 64), S("kin", 128 * b + 64, 128 * b + 128))
    ts(S("Kh"), S("Kf"), -2048.0, OP.add)

    mm([(S("P7"), L10, S("jlo", part=row)), (S("P7"), L10, S("jhi", 0, 512, part=row)), (S("P7"), L10r, onerow(512))])
    tt(S("TK", 1024 + o0, 1536 + o0), S("tki"), S("P7"), OP.add)
    peers = [c for c in T.cores if c != core]
    eng = [e for e in topo.engines(core, peers[0]) if all(e in topo.engines(core, c) for c in peers)]
    dst = [DstId(rid=topo.addr(c)[0], pnc=topo.addr(c)[1]) for c in peers]

    def send(parts, table, arr, loc, lat):
        n = len(eng) // len(parts)

        def fn():
            tr = [RemoteDMATransfer(dst_ids=dst, dma_engine_mask=sum(1 << e for e in eng[n * i:n * i + n]),
                                    remote_sem=T.sem[arr], src=p[0], dsts=[p[0]] * len(dst)) for i, p in enumerate(parts)]
            g.remote_dma_fused(tr, local_sem=T.sem[loc])
            return None
        add("g", fn, [p[1] for p in parts], [(table + "sent", 0, 1), ("orderg", 0, 1)], 0, ns=1500.0)
        add("x", None, [(table + "sent", 0, 1)], [(table + "in", 0, 1)], 0, sem=arr, cnt=n * len(parts) * len(dst),
            lat=lat, ns=0.0)
        return (loc, n * len(parts))
    tail = [send([S("NW", RT + o0, RT + o0 + 512)], "R", "aR", "sR", 7000.0),
            send([S("TK", 1024 + o0, 1536 + o0)], "TK", "aT", "sT", 16000.0),
            send([S("NW", 16 + o0, 528 + o0), S("NW", 16 + A + o0, 528 + A + o0)], "NW", "aN", "sN", 24000.0)]

    bank = [0]

    def hop(dst_, win, k0, k1, lo, hi, chain=True):
        act(S("GA", lo, hi), S(win), AF.Copy, off=S(k1, lo // 16, hi // 16))
        if chain:
            inorder("order")
        gtt(S(dst_, lo, hi), S(win), S(k0, lo // 16, hi // 16), S("GA", lo, hi), OP.max)

    def post(t, lo, hi, out, raw, relu):
        xs, m = ("X0", "M0") if t == 0 else ("X", "M")
        n = hi - lo
        pa, pb = S("P%d" % bank[0], 0, n), S("P%d" % (2 + bank[0]), 0, n)
        bank[0] ^= 1
        x, mmx, c, mp = S(xs, lo, hi), S(m, lo, hi), S("C", lo, hi), S("MP", lo, hi)
        if relu:
            mm([(pa, ident, c), (pa, S("negI"), mmx)])
            act(mp, pa, AF.Relu, bias=-2.0)
            if raw:
                mm([(pb, S("halfJ"), x), (pb, S("halfI"), mmx), (pb, S("halfI"), mp), (pb, cmag, onerow(n))])
                act(out, pb, AF.Identity, bias=-(MAGIC + OFF))
                return
            mm([(pb, ident, x), (pb, ident, mmx), (pb, ident, mp)])
            first = t == 0 and lo == 0
            act(out, pb, AF.Silu if first else AF.Identity, bias=(OFF if t == 0 else 0.0) - 0.25, scale=0.5)
            if first:
                ops[-1]["d"] += 1300.0 * PAR["cyc"]
                inorder("ordersilu")
            return
        if t == 0:
            mm([(pa, ident, mmx), (pa, c2, onerow(n))])
        else:
            mm([(pa, S("epsI"), mmx)])
        tt(mp, c, pa, OP.max)
        if not raw:
            mm([(pb, ident, x), (pb, ident, mp)])
            act(out, pb, AF.Identity, bias=(OFF if t == 0 else 0.0) - 1.25, scale=0.5)
        elif t == 0:
            mm([(pb, S("halfI"), x), (pb, S("halfI"), mp), (pb, c125, onerow(n)), (pb, cmag, onerow(n))])
            act(out, pb, AF.Identity, bias=-MAGIC)
        else:
            mm([(pb, S("halfJ"), x), (pb, S("halfI"), mp), (pb, cmag, onerow(n))])
            act(out, pb, AF.Identity, bias=-(MAGIC + OFF + 1.0))

    def cuts(lo, hi, first, last, ch):
        c = [lo]
        for f in first:
            c.append(c[-1] + f)
        end = hi - sum(last)
        while c[-1] < end:
            c.append(min(c[-1] + ch, end))
        for f in last:
            c.append(c[-1] + f)
        return list(zip(c[:-1], c[1:]))

    for t in range(3):
        Sz = V + E * t
        xs, m, k0, k1 = ("X0", "M0", "KA0", "KA1") if t == 0 else ("X", "M", "K0", "K1")
        for lo, hi in (cuts(0, Sz, (128, 256), (128,), PAR["ch"]) if t == 0 else
                       cuts(0, Sz - 2 * E, (128, 256), (), PAR["ch"]) + cuts(Sz - 2 * E, Sz, (), (128,), PAR["ch"])):
            hop(m, xs, k0, k1, lo, hi)
        if t == 2:
            for lo, hi in cuts(0, Sz, (128, 256), (128,), PAR["ch"]):
                hop("C", m, k0, k1, lo, hi)
                post(t, lo, hi, S("Y", lo, hi), True, lo in PAR["yrelu"])
                add("s", lambda lo=lo, hi=hi: g.sync.dma_start(T.y[:, lo:hi], T.Y[:, lo:hi]), [("Y", lo, hi)], [], 0,
                    sem="ys", cnt=16, lat=2200.0, ns=60.0)
            break
        n0 = Sz - E
        for lo, hi in cuts(n0, Sz, (128,), (128,), PAR["nch"]):
            hop("C", m, k0, k1, lo, hi)
            post(t, lo, hi, S("NW", XN + lo - n0, XN + hi - n0), True, False)
        for lo in range(0, n0, 256):
            hop("C", m, k0, k1, lo, lo + 256, False)
            if lo % 512:
                post(t, lo - 256, lo + 256, S("X", lo - 256, lo + 256), False, PAR["relu"][t])
        for h in range(2):
            pq = "P%d" % (6 + h)
            it = [(S(pq), L89, onerow(512)), (S(pq), L7, S("jlo", part=row)), (S(pq), L7, S("jhi", 512 * h, 512 * h + 512, part=row))]
            for b in range(2):
                for i in range(16):
                    it.append((S(pq, i, 512, 16), S3("ZZ", i, 7 - b, 135 - b), S("Kh", 64 * b + 32 * h, 64 * b + 32 * h + 32)))
            for n in range(3):
                mm(it[n:n + 1], n == 0, False)
            for n in range(3, len(it), 8):
                mm(it[n:n + 8], False, n + 8 >= len(it))
            act(S("Q", 512 * h, 512 * h + 512), S(pq), AF.Copy)
        mm([(S("P4", 0, 64), S("Zw", 15 - i, 143 - i), S("NW", XN + i, XN + E, 16)) for i in range(16)])
        for mi in range(4):
            ts(S("ci", 64 * mi, 64 * mi + 64), S("P4", 0, 64), float(97 * mi + 31 * t), OP.add)
        for lo, hi in PAR["hsplit"]:
            ts(S("cj", lo, hi), S("ci", lo, hi), 4095, OP.bitwise_and)
            ts(S("ci", lo, hi), S("cj", lo, hi), 4097.0, OP.mult)
            ts(S("cj", lo, hi), S("ci", lo, hi), 3, OP.logical_shift_right, 4095, OP.bitwise_and)
            cp(S("Lr", lo, hi), S("cj", lo, hi))
        lv = S("ones", 0, 64) if t == 0 else S("live")
        for mi in range(4):
            ts(S("pidx", 4 - mi, 320, 5), S("cj", 64 * mi, 64 * mi + 64), float(1024 + 8192 * (4 - mi)), OP.add)
            for lo, hi in ((0, 512), (512, 1024)) if mi < 3 else ((0, 512), (512, 896), (896, 1024)):
                off, xc = S("Lr", 64 * mi + lo // 16, 64 * mi + hi // 16), S("NW", XN + lo, XN + hi)
                ad = S("AD", 1024 * mi + lo, 1024 * mi + hi)
                if 2 * mi + lo // 512 < PAR["adist"][t]:
                    rg, pd = S("RG", lo, hi), S("P%d" % (4 + lo // 512))
                    act(rg, S("NW", RT, RT + A), AF.Copy, off=off)
                    withdep("Rin")
                    mm([(pd, ident, rg), (pd, S("negI"), xc)])
                    act(ad, pd, AF.Abs)
                    continue
                dd = S("D", 1024 * mi + lo, 1024 * mi + hi)
                gtt(dd, S("NW", RT, RT + A), off, xc, OP.subtract)
                withdep("Rin")
                act(ad, dd, AF.Abs)
            z = S("P5", 4 - mi, 320, 5)
            if mi == 0:
                mm([(S("P5", 0, 320, 5), ident, lv)])
            mm([(z, S("thI"), lv)] + [(z, S("Zn", 15 - i, 143 - i), S("AD", 1024 * mi + i, 1024 * mi + 1024, 16))
                                      for i in range(16)])
        scan(S("best"), S("P5", 0, 320), S("pidx"), OP.max, OP.min)
        bi, ow = S("bi"), S("ow")
        cp(bi, S("best", 4, 320, 5))
        ts(ow, bi, 9, OP.logical_shift_right, 15, OP.bitwise_and)
        for o in range(N):
            ts(S("II", 64 * o, 64 * o + 64), ow, float(o + 2), OP.is_equal)
        for lo in (0, 256):
            scan(S("IC", lo, lo + 256), S("RS64"), S("II", lo, lo + 256), OP.mult, OP.add)
        ts(S("li"), bi, 8191, OP.bitwise_and)
        cp(S("Lc"), S("li"))
        for h in range(2):
            gtt(S("G", 512 * h, 512 * h + 512), S("TK"), S("Lc", 32 * h, 32 * h + 32), S("Q", 512 * h, 512 * h + 512), OP.add)
            withdep("TKin")
        for o in range(N):
            po = S("P4", o, 512, 8)
            mm([(po, S("UT"), S("II", 64 * o, 64 * o + 64)), (po, S("BO"), S("IC", 64 * o, 64 * o + 64))])
        sm = [S("sm", 64 * n, 64 * n + 64) for n in range(10)]
        ts(sm[1], ow, 64.0, OP.mult, 1919.0 + 8192.0, OP.add)
        scan(S("own"), S("RS8"), S("P4"), OP.mult, OP.min)
        own = S("own", 7, 512, 8)
        ts(sm[2], own, -1983.5, OP.is_lt, 8192.0, OP.mult)
        tt(sm[3], own, sm[1], OP.add)
        tt(sm[4], sm[3], sm[2], OP.subtract)
        tt(sm[5], sm[4], S("dump"), OP.min)
        cp(S("Lk"), sm[5])
        tt(sm[0], S("li"), sm[2], OP.min)
        tt(sm[6], sm[0], jl, OP.max)
        cp(S("Ld"), sm[6])
        w = "W%d" % t
        add("a", lambda w=w: a.activation(T[w][:, 0:1536].indirect(T.Lk[:, 0:64]), T.G[:, 0:1024], AF.Silu),
            [("Lk", 0, 64), ("G", 0, 1024)], [(w, 0, 1536), ("ordersilu", 0, 1)], 1024 * SIG)
        ts(S("W16"), S(w, 0, 512), MAGIC - 2048.0 - LIFT, OP.add, MAGIC, OP.subtract)
        for h in range(2):
            ex, xc, src = S("EX", 512 * h, 512 * h + 512), S("XC", 512 * h, 512 * h + 512), S("NW", XN + 512 * h, XN + 512 * h + 512)
            load("s", xc, src[0], "c%d" % (2 * t + h), 2500.0, [src[1]])
            gtt(ex, S("NW", XN, RT + A), S("Ld", 32 * h, 32 * h + 32), xc, OP.add)
            withdep("Rin")
            aff(S("X", n0 + 512 * h, n0 + 512 * h + 512), ex, 0.5, OFF - 0.25)
        it = [(S("P6", 0, 64), S("ZG", 15 - i, 143 - i), S("G", i, 1024, 16)) for i in range(16)]
        for n in range(0, 16, 2):
            mm(it[n:n + 2], n == 0, n == 14)
        ts(S("qi", 128, 192), S("P6", 0, 64), -4097.0 * LIFT, OP.add)
        ts(S("qi", 0, 64), S("qi", 128, 192), 4095, OP.bitwise_and)
        ts(S("qi", 64, 128), S("qi", 128, 192), 12, OP.logical_shift_right)

        def kids(q, old, c, k, res):
            pa, pb = S("P7", 2 * c, 2 * c + 128), S("P7", 2 * c + 128, 2 * c + 256)
            s1, s2, s3 = S("s1", c, c + 128), S("s2", c, c + 128), S("s3", c, c + 128)
            tt(s1, S("V2", c, c + 128), q, OP.subtract)
            tt(s3, S("Bm", c, c + 128), q, OP.add)
            ts(pb, q, 2.5, OP.is_lt)
            ts(pa, s1, -0.5, OP.is_lt, float(Sz), OP.mult)
            tt(pb, s3, pb, OP.mult)
            tt(s2, s1, pa, OP.add)
            ts(pa, q, 0.5, OP.is_lt, float(A), OP.mult)
            tt(s1, s2, pb, OP.max)
            tt(s2, s1, pa, OP.max)
            tt(pa, s2, old, OP.subtract)
            tt(pb, S("keep", c, c + 128), pa, OP.mult)
            tt(S(res, 0, 128), s2, pb, OP.subtract)
            for b in range(2):
                cp(S("K%d" % b, k // 16, k // 16 + 64), S(res, 64 * b, 64 * b + 64))
        for b in range(2):
            aff(S("V2", 64 * b, 64 * b + 64), jl, 1.0, float(n0 + 2))
            aff(S("Bm", 64 * b, 64 * b + 64), sm[5], 2.0, float(Sz - 1))
            aff(S("keep", 64 * b, 64 * b + 64), sm[2], -1.0 / 8192.0, 1.0)
            aff(S("Bm", 128 + 64 * b, 192 + 64 * b), S("j16"), 1.0, float(Sz - 1))
        kids(S("qi", 0, 128), S("Kf"), 0, n0, "s1")

        def place(out, f):
            return [(out, S3("ZP", f, 14 - 2 * i, 142 - 2 * i), S("W16", i, 512, 8)) for i in range(8)]
        pf, pj, pt = S("P5", 0, 64), S("P5", 64, 128), S("P5", 128, 192)
        mm([(S("P5", 0, 192), one1, S("cb", 768, 960, part=row))] + place(pf, 0) + place(pj, 1) + place(pt, 4))
        mm([(S("P6", 0, 256), one1, S("cb", 768, 1024, part=row))] + place(S("P6", 0, 64), 5) + place(S("P6", 64, 128), 6),
           True, False)
        mm(place(S("P6", 128, 192), 2) + place(S("P6", 192, 256), 3), False, True)
        ts(S("keep", 128, 192), pf, S("col", 4, 5), OP.is_equal)
        ts(sm[7], pj, float(XN), OP.add)
        ts(sm[8], pt, S("col", 5, 6), OP.add)
        ts(S("live"), pf, 0.5, OP.is_gt)
        tt(sm[7], sm[7], S("keep", 128, 192), OP.mult)
        tt(sm[8], sm[8], S("live"), OP.mult)
        tt(sm[9], sm[7], sm[8], OP.max)
        cp(S("Lx"), sm[9])
        for h in range(2):
            act(S("X", Sz + 512 * h, Sz + 512 * h + 512), S("NW", 0, RT), AF.Identity, bias=OFF, off=S("Lx", 32 * h, 32 * h + 32))
            withdep("NWin")
        ts(S("keep", 192, 256), pf, S("col", 4, 5), OP.is_equal)
        for b in range(2):
            ts(S("V2", 128 + 64 * b, 192 + 64 * b), pj, float(n0 + 2), OP.add)
        kids(S("P6", 0, 128), S("P6", 128, 256), 128, Sz, "Kf")
        if t == 0:
            ts(S("Kh"), S("Kf"), -2048.0, OP.add)
    return ops, tail


ORDER = []


def depend(ops):
    hist = {}
    for n, op in enumerate(ops):
        dep = {}
        for kind, rs in (("r", op["r"]), ("w", op["w"])):
            for name, lo, hi in rs:
                ps = name in SCRATCH and SCRATCH[name][0] == "psum"
                for m, k2, l2, h2 in hist.get(name, []):
                    if m == n:
                        continue
                    if name.startswith("order") or (ps and op["e"] == "p" and ops[m]["e"] == "p"):
                        dep.setdefault(m, False)
                    elif ps and ops[m]["e"] != op["e"]:
                        dep[m] = True
                    elif l2 < hi and lo < h2 and (kind == "w" or k2 == "w"):
                        dep[m] = True
                hist.setdefault(name, []).append((n, kind, lo, hi))
        op["dep"] = dep


def plan(ops):
    latx, lats = PAR["latx"], PAR["lats"]
    depend(ops)
    succ = [[] for _ in ops]
    for n, op in enumerate(ops):
        for m in op["dep"]:
            succ[m].append(n)
    pr = [0.0] * len(ops)
    for n in range(len(ops) - 1, -1, -1):
        op = ops[n]
        pr[n] = op["d"] + max([pr[s] + (op["lat"] + latx if ops[s]["dep"][n] else 0.0) for s in succ[n]] + [op["lat"]])
    left = [len(op["dep"]) for op in ops]
    at = [0.0] * len(ops)
    ready = [n for n in range(len(ops)) if left[n] == 0]
    free = {}
    order = []
    while ready:
        best = None
        for e in sorted(set(ops[n]["e"] for n in ready)):
            mine = [n for n in ready if ops[n]["e"] == e]
            t0 = max(free.get(e, 0.0), min(at[n] for n in mine))
            n = max((n for n in mine if at[n] <= t0 + 70.0), key=lambda k: (pr[k], -k))
            if best is None or (t0, n) < best[:2]:
                best = (t0, n)
        n = best[1]
        op = ops[n]
        t0 = max(best[0], at[n])
        free[op["e"]] = t0 + op["d"]
        order.append(n)
        ready.remove(n)
        for s in succ[n]:
            gap = 0.0
            if ops[s]["dep"][n]:
                gap = op["lat"] + (lats if ops[s]["e"] == op["e"] else latx)
            at[s] = max(at[s], t0 + op["d"] + gap)
            left[s] -= 1
            if left[s] == 0:
                ready.append(s)
    return improve(ops, order)


def improve(ops, order):
    nops = len(ops)
    figs = [(1.0, PAR["latx"], PAR["lats"]), (0.85, 2.0 * PAR["latx"], 2.5 * PAR["lats"])]
    anc = [0] * nops
    deps = []
    for n, op in enumerate(ops):
        keep, cover = [], 0
        for m in sorted(op["dep"], reverse=True):
            if not cover >> m & 1 or ops[m]["lat"]:
                keep.append(m)
            if op["dep"][m] or not ops[m]["lat"]:
                cover |= anc[m]
            anc[n] |= anc[m] | 1 << m
        deps.append([(m, op["dep"][m], ops[m]["e"] == op["e"]) for m in keep])
    edge = [[[(m, (ops[m]["lat"] + (ls if same else lx)) if w else 0.0) for m, w, same in deps[n]] for n in range(nops)]
            for _, lx, ls in figs]
    dur = [[op["d"] * f for op in ops] for f, _, _ in figs]
    eng = [op["e"] for op in ops]
    lat = [op["lat"] for op in ops]

    def run(seq, k):
        free, end, why = {}, [0.0] * nops, [-1] * nops
        ed, du = edge[k], dur[k]
        for n in seq:
            t, w = free.get(eng[n], (0.0, -1))
            for m, gap in ed[n]:
                if end[m] + gap > t:
                    t, w = end[m] + gap, m
            end[n] = t + du[n]
            why[n] = w
            free[eng[n]] = (end[n], n)
        last = max(range(nops), key=lambda n: end[n] + lat[n])
        return end[last] + lat[last], end, why, last

    def moved(seq, n, m):
        i, j = seq.index(m), seq.index(n)
        if i >= j or anc[n] >> m & 1:
            return None
        mid = seq[i:j]
        return seq[:i] + [x for x in mid if anc[n] >> x & 1] + [n] + [x for x in mid if not anc[n] >> x & 1] + seq[j + 1:]

    def held(seq, m, n):
        i, j = seq.index(m), seq.index(n)
        if i >= j or anc[n] >> m & 1:
            return None
        mid = seq[i + 1:j + 1]
        return seq[:i] + [x for x in mid if not anc[x] >> m & 1] + [m] + [x for x in mid if anc[x] >> m & 1] + seq[j + 1:]

    rng = np.random.default_rng(PAR["seed"])
    seq = list(order)
    res = [run(seq, k) for k in range(len(figs))]
    cur = sum(r[0] for r in res)
    best, top = cur, seq
    for it in range(PAR["iters"]):
        _, end, why, n = res[int(rng.integers(len(figs)))]
        path = []
        while n >= 0:
            if why[n] >= 0 and eng[why[n]] == eng[n] and why[n] not in ops[n]["dep"]:
                path.append(n)
            n = why[n]
        if not path:
            break
        n = path[int(rng.integers(len(path)))]
        mine = [x for x in seq if eng[x] == eng[n]]
        i = mine.index(n)
        if rng.random() < 0.5:
            new = moved(seq, n, mine[max(0, i - int(rng.geometric(0.5)))])
        else:
            new = held(seq, mine[max(0, i - int(rng.geometric(0.6)))], mine[min(len(mine) - 1, i - 1 + int(rng.geometric(0.3)))])
        if new is None:
            continue
        r2 = [run(new, k) for k in range(len(figs))]
        c2 = sum(r[0] for r in r2)
        if c2 <= cur + PAR["temp"] * (1.0 - it / PAR["iters"]) * rng.random():
            seq, res, cur = new, r2, c2
            if cur < best:
                best, top = cur, seq
    end = run(top, 0)[1]
    return top, {n: end[n] - dur[0][n] for n in top}


def rank_program(g, core, T, topo):
    if T.rank_of(core) is None:
        return
    ops, tail = build(g, core, T, topo)
    if not ORDER:
        ORDER.extend(plan(ops)[0])
    order = ORDER
    depend(ops)
    queue = {"v": g.vector, "a": g.scalar, "p": g.tensor, "g": g, "s": g.sync}
    esem = {"v": "ev", "a": "ea", "p": "ep", "g": "eg"}
    pos = {n: i for i, n in enumerate(order)}
    need = {}
    for n in order:
        last, dm = {}, []
        if ops[n]["e"] != "x":
            for m, wait in ops[n]["dep"].items():
                if not wait:
                    continue
                if ops[m]["sem"] is not None:
                    dm.append(m)
                elif ops[m]["e"] not in last or pos[m] > pos[last[ops[m]["e"]]]:
                    last[ops[m]["e"]] = m
        need[n] = (last, dm)
    seen = {}
    marked = set()
    for n in order:
        e = ops[n]["e"]
        for e2, m in list(need[n][0].items()):
            if seen.get((e, e2), -1) >= pos[m]:
                del need[n][0][e2]
            else:
                seen[(e, e2)] = pos[m]
                marked.add(m)
    count, value, waited, total = {}, {}, set(), {}
    for n in order:
        op = ops[n]
        e = op["e"]
        if op["sem"] is not None:
            total[op["sem"]] = total.get(op["sem"], 0) + op["cnt"]
        if e == "x":
            continue
        for e2, m in need[n][0].items():
            queue[e].wait_ge(T.sem[esem[e2]], value[m])
        for m in need[n][1]:
            if (e, m) not in waited:
                waited.add((e, m))
                queue[e].wait_ge(T.sem[ops[m]["sem"]], ops[m]["cnt"])
        ins = op["fn"]()
        if op["sem"] is not None:
            ins.then_inc(T.sem[op["sem"]], op["cnt"])
        elif n in marked:
            count[e] = count.get(e, 0) + 1
            value[n] = count[e]
            ins.then_inc(T.sem[esem[e]], 1)
    for name, c in tail:
        g.wait_ge(T.sem[name], c)
    g.sync.wait_ge(T.sem.ys, total["ys"])
